import numpy as np, ml_dtypes
CORES = [15,47,79,175,207]
N = 5
TK = 512
def setup_inputs(rng):
    return {"b": rng.standard_normal((N, 128, TK), dtype=np.float32).astype(ml_dtypes.bfloat16), "l": (rng.standard_normal((N, 128, N * 128), dtype=np.float32) / 16).astype(ml_dtypes.bfloat16)}
def setup_inputs_big(rng):
    d = setup_inputs(rng)
    for k in ("b",): d[k] = (d[k].astype(np.float32) * 1048576.0).astype(d[k].dtype)
    return d
def setup_inputs_small(rng):
    d = setup_inputs(rng)
    for k in ("b",): d[k] = (d[k].astype(np.float32) * (1 / 1048576.0)).astype(d[k].dtype)
    return d
def setup_inputs_apart(rng):
    d = setup_inputs(rng)
    f = (10.0 ** rng.permutation(np.linspace(-1.5, 1.5, N))).astype(np.float32).reshape(N, 1, 1)
    for k in ("b",): d[k] = (d[k].astype(np.float32) * f).astype(d[k].dtype)
    return d
def reference(b, l):
    B, L = b.astype(np.float64), l.astype(np.float64)
    y = np.zeros((N, 128, TK))
    for r in range(N):
        acc = B[r].copy()
        for s in range(r):
            acc -= L[s][:, 128 * r:128 * r + 128].T @ y[s]
        y[r] = acc
    return {"y": y.astype(ml_dtypes.bfloat16)}

@@ -1,0 +1,98 @@
+from concourse.mybir import AluOpType
+
+N = 5
+W = 512
+TW = 128
+FILL = 2
+
+SEND_ORDER = {0: [4, 3, 2, 1], 1: [4, 3, 2], 2: [3, 4], 3: [4]}
+
+SCRATCH = {"own": ("sbuf", [128, W + TW * (N - 1)], "bfloat16")}
+for _s in range(N - 1):
+    SCRATCH["land%d" % _s] = ("sbuf", [128, W + TW * (N - 1 - _s)], "bfloat16")
+for _r in range(1, N):
+    SCRATCH["y%d" % _r] = ("sbuf", [128, W], "bfloat16")
+    SCRATCH["p%d" % _r] = ("psum", [128, W], "float32")
+
+SEMAPHORES = (["ld", "sent", "st"] + ["arr%d" % s for s in range(N - 1)]
+              + ["pm%d" % r for r in range(1, N)] + ["vs%d" % r for r in range(1, N)])
+
+
+def _count(mask):
+    return bin(mask).count("1")
+
+
+def rank_program(g, core, T, topo):
+    me = T.rank_of(core)
+    if me is None:
+        return
+    sem = T.sem
+    cores = T.cores
+
+    g.sync.dma_start(T.own[:, 0:W], T.b[:]).then_inc(sem.ld, 16)
+    loaded = 16
+    if me < N - 1:
+        g.scalar.dma_start(T.own[:, W:W + TW * (N - 1 - me)], T.l[:, TW * (me + 1):TW * N]).then_inc(sem.ld, 16)
+        loaded += 16
+    if me == 0:
+        g.scalar.dma_start(T.y[:], T.b[:]).then_inc(sem.st, 16)
+
+    if me < N - 1:
+        g.wait_ge(sem.ld, loaded)
+        left = 0
+        for d in SEND_ORDER[me]:
+            dst = cores[d]
+            rid, pid = topo.addr(dst, core)
+            mask = topo.mask(core, dst)
+            w = W + TW * (d - me)
+            g.remote_dma(T["land%d" % me][:, 0:w], T.own[:, 0:w], sem["arr%d" % me], sem.sent, pid, rid, mask)
+            left += _count(mask)
+        g.wait_ge(sem.sent, left)
+
+    if me == 0:
+        g.scalar.wait_ge(sem.st, 16)
+        return
+
+    def arrived(s):
+        return _count(topo.mask(cores[s], core))
+
+    def tile(r, s):
+        c = W + TW * (r - s - 1)
+        return T["land%d" % s][:, c:c + TW]
+
+    def yv(s):
+        return T.land0[:, 0:W] if s == 0 else T["y%d" % s][:]
+
+    opened = set()
+
+    def mm(r, s):
+        g.tensor.matmul(T["p%d" % r][:], tile(r, s), yv(s), start=(r not in opened), stop=(s == r - 1)).then_inc(
+            sem["pm%d" % r], 1)
+        opened.add(r)
+
+    later = [(r, s) for r in range(2, me + 1) for s in range(r - 1)]
+    for s in range(me):
+        g.tensor.wait_ge(sem["arr%d" % s], arrived(s))
+        if s > 0:
+            g.tensor.wait_ge(sem["vs%d" % s], 1)
+        mm(s + 1, s)
+        n = 0
+        for (r, q) in list(later):
+            if q <= s and (r == s + 2 or n < FILL):
+                mm(r, q)
+                later.remove((r, q))
+                n += 1
+
+    for r in range(1, me + 1):
+        if r == me:
+            g.vector.wait_ge(sem.ld, loaded)
+            b = T.own[:, 0:W]
+        else:
+            g.vector.wait_ge(sem["arr%d" % r], arrived(r))
+            b = T["land%d" % r][:, 0:W]
+        g.vector.wait_ge(sem["pm%d" % r], r)
+        g.vector.tensor_tensor(T["y%d" % r][:], b, T["p%d" % r][:], AluOpType.subtract).then_inc(sem["vs%d" % r], 1)
+
+    g.sync.wait_ge(sem["vs%d" % me], 1)
+    g.sync.dma_start(T.y[:], T["y%d" % me][:]).then_inc(sem.st, 16)
+    g.sync.wait_ge(sem.st, 16)

@@ -3,96 +3,163 @@ from concourse.mybir import AluOpType
 N = 5
 W = 512
 TW = 128
-FILL = 2
+HW = 256
+WORLD = 256
 
-SEND_ORDER = {0: [4, 3, 2, 1], 1: [4, 3, 2], 2: [3, 4], 3: [4]}
+DIRECT = {0: [4, 3], 1: [3, 2], 2: [3], 3: [4]}
+RELAY = {0: [2, 1], 1: [4], 2: [4], 3: []}
 
-SCRATCH = {"own": ("sbuf", [128, W + TW * (N - 1)], "bfloat16")}
+SCRATCH = {"own": ("sbuf", [128, W + TW * (N - 1)], "bfloat16"),
+           "ones": ("sbuf", [128, TW], "bfloat16"),
+           "ident": ("sbuf", [128, TW], "bfloat16"),
+           "yo": ("sbuf", [128, W], "bfloat16"),
+           "acc0": ("psum", [128, W], "float32"),
+           "acc1": ("psum", [128, W], "float32")}
 for _s in range(N - 1):
     SCRATCH["land%d" % _s] = ("sbuf", [128, W + TW * (N - 1 - _s)], "bfloat16")
-for _r in range(1, N):
-    SCRATCH["y%d" % _r] = ("sbuf", [128, W], "bfloat16")
-    SCRATCH["p%d" % _r] = ("psum", [128, W], "float32")
+for _s in range(N - 2):
+    SCRATCH["tT%d" % _s] = ("sbuf", [128, TW * (N - 2 - _s)], "bfloat16")
+    SCRATCH["P%d" % _s] = ("sbuf", [128, TW], "bfloat16")
+    SCRATCH["pT%d" % _s] = ("psum", [128, W], "float32")
+    SCRATCH["pc%d" % _s] = ("psum", [128, W], "float32")
 
-SEMAPHORES = (["ld", "sent", "st"] + ["arr%d" % s for s in range(N - 1)]
-              + ["pm%d" % r for r in range(1, N)] + ["vs%d" % r for r in range(1, N)])
+SEMAPHORES = (["ldT", "ldB", "fT", "fB", "sent", "st", "on", "idn", "am0", "am1", "vs"]
+              + [p + "%d" % s for s in range(N - 1) for p in ("arrT", "arrB")]
+              + [p + "%d" % s for s in range(N - 2) for p in ("tp", "tc", "pm", "pv")])
 
 
 def _count(mask):
     return bin(mask).count("1")
 
 
+def _helper(topo, cores, s):
+    c = cores[s]
+    for x in range(WORLD):
+        if (x not in cores and topo.host(x) == topo.host(c) and topo.chip(x) == topo.chip(c)
+                and topo.die(x) != topo.die(c) and all(topo.may_write(x, cores[d]) for d in RELAY[s])):
+            return x
+    return None
+
+
+def _serve(g, core, T, topo, s, dests, part):
+    n = 0
+    for d in dests:
+        dst = T.cores[d]
+        rid, pid = topo.addr(dst, core)
+        mask = topo.mask(core, dst)
+        lo, hi = (W, W + TW * (d - s)) if part == "T" else (0, W)
+        g.remote_dma(T["land%d" % s][:, lo:hi], T.own[:, lo:hi], T.sem["arr%s%d" % (part, s)], T.sem.sent, pid, rid,
+                     mask)
+        n += _count(mask)
+    return n
+
+
 def rank_program(g, core, T, topo):
-    me = T.rank_of(core)
-    if me is None:
-        return
     sem = T.sem
-    cores = T.cores
+    cores = list(T.cores)
+    me = T.rank_of(core)
 
-    g.sync.dma_start(T.own[:, 0:W], T.b[:]).then_inc(sem.ld, 16)
-    loaded = 16
+    if me is None:
+        for s in range(N - 1):
+            if RELAY[s] and _helper(topo, cores, s) == core:
+                fed = _count(topo.mask(cores[s], core) & ~topo.mask(cores[s], cores[RELAY[s][0]]))
+                g.wait_ge(sem.fT, fed)
+                left = _serve(g, core, T, topo, s, RELAY[s], "T")
+                g.wait_ge(sem.fB, fed)
+                left += _serve(g, core, T, topo, s, RELAY[s], "B")
+                g.wait_ge(sem.sent, left)
+        return
+
+    d = me
     if me < N - 1:
-        g.scalar.dma_start(T.own[:, W:W + TW * (N - 1 - me)], T.l[:, TW * (me + 1):TW * N]).then_inc(sem.ld, 16)
-        loaded += 16
-    if me == 0:
-        g.scalar.dma_start(T.y[:], T.b[:]).then_inc(sem.st, 16)
+        g.scalar.dma_start(T.own[:, W:W + TW * (N - 1 - me)], T.l[:, TW * (me + 1):TW * N]).then_inc(sem.ldT, 16)
+    g.sync.dma_start(T.own[:, 0:W], T.b[:]).then_inc(sem.ldB, 16)
+
+    if d >= 2:
+        g.vector.memset(T.ones[:], 1.0).then_inc(sem.on, 1)
+        g.wait_ge(sem.on, 1)
+        g.affine_select(T.ident[:], T.ones[:], [[-1, TW]], AluOpType.is_equal, 0.0, 0, 1).then_inc(sem.idn, 1)
 
     if me < N - 1:
-        g.wait_ge(sem.ld, loaded)
         left = 0
-        for d in SEND_ORDER[me]:
-            dst = cores[d]
-            rid, pid = topo.addr(dst, core)
-            mask = topo.mask(core, dst)
-            w = W + TW * (d - me)
-            g.remote_dma(T["land%d" % me][:, 0:w], T.own[:, 0:w], sem["arr%d" % me], sem.sent, pid, rid, mask)
-            left += _count(mask)
+        hc = _helper(topo, cores, me) if RELAY[me] else None
+        if hc is not None:
+            hrid, hpid = topo.addr(hc, core)
+            hmask = topo.mask(core, hc) & ~topo.mask(core, cores[RELAY[me][0]])
+            thi = W + TW * (max(RELAY[me]) - me)
+        g.wait_ge(sem.ldT, 16)
+        if hc is not None:
+            g.remote_dma(T.own[:, W:thi], T.own[:, W:thi], sem.fT, sem.sent, hpid, hrid, hmask)
+            left += _count(hmask)
+        left += _serve(g, core, T, topo, me, DIRECT[me], "T")
+        g.wait_ge(sem.ldB, 16)
+        if hc is not None:
+            g.remote_dma(T.own[:, 0:W], T.own[:, 0:W], sem.fB, sem.sent, hpid, hrid, hmask)
+            left += _count(hmask)
+        left += _serve(g, core, T, topo, me, DIRECT[me], "B")
         g.wait_ge(sem.sent, left)
 
     if me == 0:
+        g.scalar.wait_ge(sem.sent, left)
+        g.scalar.dma_start(T.y[:], T.own[:, 0:W]).then_inc(sem.st, 16)
         g.scalar.wait_ge(sem.st, 16)
         return
 
     def arrived(s):
-        return _count(topo.mask(cores[s], core))
+        src = cores[s] if d in DIRECT[s] else _helper(topo, cores, s)
+        return _count(topo.mask(src, core))
 
     def tile(r, s):
         c = W + TW * (r - s - 1)
         return T["land%d" % s][:, c:c + TW]
 
-    def yv(s):
-        return T.land0[:, 0:W] if s == 0 else T["y%d" % s][:]
+    def P(s):
+        return tile(d, s) if s == d - 1 else T["P%d" % s][:]
 
-    opened = set()
+    te, ve = g.tensor, g.vector
+    if d >= 2:
+        te.wait_ge(sem.idn, 1)
+        for s in range(d - 2, -1, -1):
+            te.wait_ge(sem["arrT%d" % s], arrived(s))
+            for q in range(s + 1, d):
+                c = (q - s - 1) * TW
+                te.matmul(T["pT%d" % s][:, c:c + TW], tile(q, s), T.ident[:], start=True, stop=True).then_inc(
+                    sem["tp%d" % s], 1)
+        te.wait_ge(sem["arrT%d" % (d - 1)], arrived(d - 1))
+        for q in range(d - 1, 0, -1):
+            if q < d - 1:
+                te.wait_ge(sem["pv%d" % q], 1)
+            for s in range(q - 1, -1, -1):
+                if q == d - 1:
+                    te.wait_ge(sem["tc%d" % s], 1)
+                c = (q - s - 1) * TW
+                te.matmul(T["pc%d" % s][:, 0:TW], T["tT%d" % s][:, c:c + TW], P(q), start=(q == d - 1),
+                          stop=(q == s + 1)).then_inc(sem["pm%d" % s], 1)
+        for s in range(d - 2, -1, -1):
+            n = (d - 1 - s) * TW
+            ve.wait_ge(sem["tp%d" % s], d - 1 - s)
+            ve.tensor_copy(T["tT%d" % s][:, 0:n], T["pT%d" % s][:, 0:n]).then_inc(sem["tc%d" % s], 1)
+        for s in range(d - 2, -1, -1):
+            ve.wait_ge(sem["arrT%d" % s], arrived(s))
+            ve.wait_ge(sem["pm%d" % s], d - 1 - s)
+            ve.tensor_tensor(T["P%d" % s][:], tile(d, s), T["pc%d" % s][:, 0:TW], AluOpType.subtract).then_inc(
+                sem["pv%d" % s], 1)
 
-    def mm(r, s):
-        g.tensor.matmul(T["p%d" % r][:], tile(r, s), yv(s), start=(r not in opened), stop=(s == r - 1)).then_inc(
-            sem["pm%d" % r], 1)
-        opened.add(r)
+    for i, s in enumerate(range(d - 1, -1, -1)):
+        te.wait_ge(sem["arrT%d" % s], arrived(s))
+        te.wait_ge(sem["arrB%d" % s], arrived(s))
+        if s <= d - 2:
+            te.wait_ge(sem["pv%d" % s], 1)
+        for h in range(2):
+            te.matmul(T["acc%d" % h][:, 0:HW], P(s), T["land%d" % s][:, h * HW:(h + 1) * HW], start=(i == 0),
+                      stop=(i == d - 1)).then_inc(sem["am%d" % h], 1)
 
-    later = [(r, s) for r in range(2, me + 1) for s in range(r - 1)]
-    for s in range(me):
-        g.tensor.wait_ge(sem["arr%d" % s], arrived(s))
-        if s > 0:
-            g.tensor.wait_ge(sem["vs%d" % s], 1)
-        mm(s + 1, s)
-        n = 0
-        for (r, q) in list(later):
-            if q <= s and (r == s + 2 or n < FILL):
-                mm(r, q)
-                later.remove((r, q))
-                n += 1
+    ve.wait_ge(sem.ldB, 16)
+    for h in range(2):
+        ve.wait_ge(sem["am%d" % h], d)
+        ve.tensor_tensor(T.yo[:, h * HW:(h + 1) * HW], T.own[:, h * HW:(h + 1) * HW], T["acc%d" % h][:, 0:HW],
+                         AluOpType.subtract).then_inc(sem.vs, 1)
 
-    for r in range(1, me + 1):
-        if r == me:
-            g.vector.wait_ge(sem.ld, loaded)
-            b = T.own[:, 0:W]
-        else:
-            g.vector.wait_ge(sem["arr%d" % r], arrived(r))
-            b = T["land%d" % r][:, 0:W]
-        g.vector.wait_ge(sem["pm%d" % r], r)
-        g.vector.tensor_tensor(T["y%d" % r][:], b, T["p%d" % r][:], AluOpType.subtract).then_inc(sem["vs%d" % r], 1)
-
-    g.sync.wait_ge(sem["vs%d" % me], 1)
-    g.sync.dma_start(T.y[:], T["y%d" % me][:]).then_inc(sem.st, 16)
+    g.sync.wait_ge(sem.vs, 2)
+    g.sync.dma_start(T.y[:], T.yo[:]).then_inc(sem.st, 16)
     g.sync.wait_ge(sem.st, 16)

@@ -6,26 +6,31 @@ TW = 128
 HW = 256
 WORLD = 256
 
-DIRECT = {0: [4, 3], 1: [3, 2], 2: [3], 3: [4]}
-RELAY = {0: [2, 1], 1: [4], 2: [4], 3: []}
+BD = {0: [4, 3], 1: [3, 2], 2: [4], 3: []}
+BR = {0: [2, 1], 1: [4], 2: [3], 3: [4]}
 
 SCRATCH = {"own": ("sbuf", [128, W + TW * (N - 1)], "bfloat16"),
            "ones": ("sbuf", [128, TW], "bfloat16"),
+           "zero": ("sbuf", [128, TW], "bfloat16"),
            "ident": ("sbuf", [128, TW], "bfloat16"),
            "yo": ("sbuf", [128, W], "bfloat16"),
            "acc0": ("psum", [128, W], "float32"),
            "acc1": ("psum", [128, W], "float32")}
 for _s in range(N - 1):
-    SCRATCH["land%d" % _s] = ("sbuf", [128, W + TW * (N - 1 - _s)], "bfloat16")
-for _s in range(N - 2):
-    SCRATCH["tT%d" % _s] = ("sbuf", [128, TW * (N - 2 - _s)], "bfloat16")
-    SCRATCH["P%d" % _s] = ("sbuf", [128, TW], "bfloat16")
-    SCRATCH["pT%d" % _s] = ("psum", [128, W], "float32")
-    SCRATCH["pc%d" % _s] = ("psum", [128, W], "float32")
+    SCRATCH["lb%d" % _s] = ("sbuf", [128, W], "bfloat16")
+    SCRATCH["lp%d" % _s] = ("sbuf", [128, TW], "bfloat16")
+for _q in range(1, N - 1):
+    SCRATCH["rt%d" % _q] = ("sbuf", [128, TW * (N - 1 - _q)], "bfloat16")
+    SCRATCH["Nn%d" % _q] = ("sbuf", [128, TW], "bfloat16")
+    SCRATCH["pn%d" % _q] = ("psum", [128, W], "float32")
+for _d in range(2, N):
+    SCRATCH["Pp%d" % _d] = ("sbuf", [128, TW], "bfloat16")
+    SCRATCH["pp%d" % _d] = ("psum", [128, W], "float32")
 
-SEMAPHORES = (["ldT", "ldB", "fT", "fB", "sent", "st", "on", "idn", "am0", "am1", "vs"]
-              + [p + "%d" % s for s in range(N - 1) for p in ("arrT", "arrB")]
-              + [p + "%d" % s for s in range(N - 2) for p in ("tp", "tc", "pm", "pv")])
+SEMAPHORES = (["ldT", "ldB", "fT", "fB", "sent", "st", "on", "zr", "idn", "am0", "am1", "vs"]
+              + [p + "%d" % s for s in range(N - 1) for p in ("arrB", "arrP")]
+              + [p + "%d" % q for q in range(1, N - 1) for p in ("arrR", "nm", "nv")]
+              + [p + "%d" % d for d in range(2, N) for p in ("pm", "pv")])
 
 
 def _count(mask):
@@ -36,22 +41,9 @@ def _helper(topo, cores, s):
     c = cores[s]
     for x in range(WORLD):
         if (x not in cores and topo.host(x) == topo.host(c) and topo.chip(x) == topo.chip(c)
-                and topo.die(x) != topo.die(c) and all(topo.may_write(x, cores[d]) for d in RELAY[s])):
+                and topo.die(x) != topo.die(c) and all(topo.may_write(x, cores[d]) for d in BR[s] + [s + 1])):
             return x
     return None
-
-
-def _serve(g, core, T, topo, s, dests, part):
-    n = 0
-    for d in dests:
-        dst = T.cores[d]
-        rid, pid = topo.addr(dst, core)
-        mask = topo.mask(core, dst)
-        lo, hi = (W, W + TW * (d - s)) if part == "T" else (0, W)
-        g.remote_dma(T["land%d" % s][:, lo:hi], T.own[:, lo:hi], T.sem["arr%s%d" % (part, s)], T.sem.sent, pid, rid,
-                     mask)
-        n += _count(mask)
-    return n
 
 
 def rank_program(g, core, T, topo):
@@ -59,45 +51,91 @@ def rank_program(g, core, T, topo):
     cores = list(T.cores)
     me = T.rank_of(core)
 
+    def send(d, out_ap, in_ap, rsem):
+        rid, pid = topo.addr(cores[d], core)
+        mask = topo.mask(core, cores[d])
+        g.remote_dma(out_ap, in_ap, rsem, sem.sent, pid, rid, mask)
+        return _count(mask)
+
     if me is None:
         for s in range(N - 1):
-            if RELAY[s] and _helper(topo, cores, s) == core:
-                fed = _count(topo.mask(cores[s], core) & ~topo.mask(cores[s], cores[RELAY[s][0]]))
+            if _helper(topo, cores, s) == core:
+                fed = _count(topo.mask(cores[s], core) & ~topo.mask(cores[s], cores[s + 1]))
                 g.wait_ge(sem.fT, fed)
-                left = _serve(g, core, T, topo, s, RELAY[s], "T")
+                left = send(s + 1, T["lp%d" % s][:], T.own[:, W:W + TW], sem["arrP%d" % s])
                 g.wait_ge(sem.fB, fed)
-                left += _serve(g, core, T, topo, s, RELAY[s], "B")
+                for d in BR[s]:
+                    left += send(d, T["lb%d" % s][:], T.own[:, 0:W], sem["arrB%d" % s])
                 g.wait_ge(sem.sent, left)
         return
 
-    d = me
+    s = me
+    te, ve = g.tensor, g.vector
+    chain = me <= N - 3
+
     if me < N - 1:
         g.scalar.dma_start(T.own[:, W:W + TW * (N - 1 - me)], T.l[:, TW * (me + 1):TW * N]).then_inc(sem.ldT, 16)
     g.sync.dma_start(T.own[:, 0:W], T.b[:]).then_inc(sem.ldB, 16)
 
-    if d >= 2:
-        g.vector.memset(T.ones[:], 1.0).then_inc(sem.on, 1)
+    if chain:
+        ve.memset(T.ones[:], 1.0).then_inc(sem.on, 1)
+        ve.memset(T.zero[:], 0.0).then_inc(sem.zr, 1)
         g.wait_ge(sem.on, 1)
         g.affine_select(T.ident[:], T.ones[:], [[-1, TW]], AluOpType.is_equal, 0.0, 0, 1).then_inc(sem.idn, 1)
 
+    left = 0
     if me < N - 1:
-        left = 0
-        hc = _helper(topo, cores, me) if RELAY[me] else None
-        if hc is not None:
-            hrid, hpid = topo.addr(hc, core)
-            hmask = topo.mask(core, hc) & ~topo.mask(core, cores[RELAY[me][0]])
-            thi = W + TW * (max(RELAY[me]) - me)
+        hc = _helper(topo, cores, me)
+        hrid, hpid = topo.addr(hc, core)
+        hmask = topo.mask(core, hc) & ~topo.mask(core, cores[me + 1])
         g.wait_ge(sem.ldT, 16)
-        if hc is not None:
-            g.remote_dma(T.own[:, W:thi], T.own[:, W:thi], sem.fT, sem.sent, hpid, hrid, hmask)
-            left += _count(hmask)
-        left += _serve(g, core, T, topo, me, DIRECT[me], "T")
+        for lo in range(me):
+            left += send(lo, T["rt%d" % me][:], T.own[:, W:W + TW * (N - 1 - me)], sem["arrR%d" % me])
+        g.remote_dma(T.own[:, W:W + TW], T.own[:, W:W + TW], sem.fT, sem.sent, hpid, hrid, hmask)
+        left += _count(hmask)
         g.wait_ge(sem.ldB, 16)
-        if hc is not None:
-            g.remote_dma(T.own[:, 0:W], T.own[:, 0:W], sem.fB, sem.sent, hpid, hrid, hmask)
-            left += _count(hmask)
-        left += _serve(g, core, T, topo, me, DIRECT[me], "B")
+        g.remote_dma(T.own[:, 0:W], T.own[:, 0:W], sem.fB, sem.sent, hpid, hrid, hmask)
+        left += _count(hmask)
+        for d in BD[me]:
+            left += send(d, T["lb%d" % me][:], T.own[:, 0:W], sem["arrB%d" % me])
+        for d in range(me + 2, N):
+            g.wait_ge(sem["pv%d" % d], 1)
+            left += send(d, T["lp%d" % me][:], T["Pp%d" % d][:], sem["arrP%d" % me])
         g.wait_ge(sem.sent, left)
+
+    def tile(d, q):
+        if q == me:
+            c = W + TW * (d - me - 1)
+            return T.own[:, c:c + TW]
+        c = TW * (d - q - 1)
+        return T["rt%d" % q][:, c:c + TW]
+
+    if chain:
+        te.wait_ge(sem.idn, 1)
+        te.wait_ge(sem.ldT, 16)
+        for q in range(s + 1, N - 1):
+            te.matmul(T["pn%d" % q][:, 0:TW], tile(q, s), T.ident[:], start=True, stop=(q == s + 1)).then_inc(
+                sem["nm%d" % q], 1)
+        for p in range(s + 1, N - 1):
+            te.wait_ge(sem["nv%d" % p], 1)
+            te.wait_ge(sem["arrR%d" % p], _count(topo.mask(cores[p], core)))
+            for k in range(p + 1, N):
+                if k < N - 1:
+                    te.matmul(T["pn%d" % k][:, 0:TW], tile(k, p), T["Nn%d" % p][:], start=False,
+                              stop=(k == p + 1)).then_inc(sem["nm%d" % k], 1)
+                te.matmul(T["pp%d" % k][:, 0:TW], T["Nn%d" % p][:], tile(k, p), start=(p == s + 1),
+                          stop=(k == p + 1)).then_inc(sem["pm%d" % k], 1)
+        ve.wait_ge(sem.zr, 1)
+        ve.wait_ge(sem.ldT, 16)
+        for k in range(s + 1, N):
+            if k < N - 1:
+                ve.wait_ge(sem["nm%d" % k], k - s)
+                ve.tensor_tensor(T["Nn%d" % k][:], T.zero[:], T["pn%d" % k][:, 0:TW], AluOpType.subtract).then_inc(
+                    sem["nv%d" % k], 1)
+            if k > s + 1:
+                ve.wait_ge(sem["pm%d" % k], k - 1 - s)
+                ve.tensor_tensor(T["Pp%d" % k][:], tile(k, s), T["pp%d" % k][:, 0:TW], AluOpType.add).then_inc(
+                    sem["pv%d" % k], 1)
 
     if me == 0:
         g.scalar.wait_ge(sem.sent, left)
@@ -105,53 +143,14 @@ def rank_program(g, core, T, topo):
         g.scalar.wait_ge(sem.st, 16)
         return
 
-    def arrived(s):
-        src = cores[s] if d in DIRECT[s] else _helper(topo, cores, s)
-        return _count(topo.mask(src, core))
-
-    def tile(r, s):
-        c = W + TW * (r - s - 1)
-        return T["land%d" % s][:, c:c + TW]
-
-    def P(s):
-        return tile(d, s) if s == d - 1 else T["P%d" % s][:]
-
-    te, ve = g.tensor, g.vector
-    if d >= 2:
-        te.wait_ge(sem.idn, 1)
-        for s in range(d - 2, -1, -1):
-            te.wait_ge(sem["arrT%d" % s], arrived(s))
-            for q in range(s + 1, d):
-                c = (q - s - 1) * TW
-                te.matmul(T["pT%d" % s][:, c:c + TW], tile(q, s), T.ident[:], start=True, stop=True).then_inc(
-                    sem["tp%d" % s], 1)
-        te.wait_ge(sem["arrT%d" % (d - 1)], arrived(d - 1))
-        for q in range(d - 1, 0, -1):
-            if q < d - 1:
-                te.wait_ge(sem["pv%d" % q], 1)
-            for s in range(q - 1, -1, -1):
-                if q == d - 1:
-                    te.wait_ge(sem["tc%d" % s], 1)
-                c = (q - s - 1) * TW
-                te.matmul(T["pc%d" % s][:, 0:TW], T["tT%d" % s][:, c:c + TW], P(q), start=(q == d - 1),
-                          stop=(q == s + 1)).then_inc(sem["pm%d" % s], 1)
-        for s in range(d - 2, -1, -1):
-            n = (d - 1 - s) * TW
-            ve.wait_ge(sem["tp%d" % s], d - 1 - s)
-            ve.tensor_copy(T["tT%d" % s][:, 0:n], T["pT%d" % s][:, 0:n]).then_inc(sem["tc%d" % s], 1)
-        for s in range(d - 2, -1, -1):
-            ve.wait_ge(sem["arrT%d" % s], arrived(s))
-            ve.wait_ge(sem["pm%d" % s], d - 1 - s)
-            ve.tensor_tensor(T["P%d" % s][:], tile(d, s), T["pc%d" % s][:, 0:TW], AluOpType.subtract).then_inc(
-                sem["pv%d" % s], 1)
-
-    for i, s in enumerate(range(d - 1, -1, -1)):
-        te.wait_ge(sem["arrT%d" % s], arrived(s))
-        te.wait_ge(sem["arrB%d" % s], arrived(s))
-        if s <= d - 2:
-            te.wait_ge(sem["pv%d" % s], 1)
+    d = me
+    for i, r in enumerate(range(d - 1, -1, -1)):
+        psrc = _helper(topo, cores, r) if d == r + 1 else cores[r]
+        bsrc = cores[r] if d in BD[r] else _helper(topo, cores, r)
+        te.wait_ge(sem["arrP%d" % r], _count(topo.mask(psrc, core)))
+        te.wait_ge(sem["arrB%d" % r], _count(topo.mask(bsrc, core)))
         for h in range(2):
-            te.matmul(T["acc%d" % h][:, 0:HW], P(s), T["land%d" % s][:, h * HW:(h + 1) * HW], start=(i == 0),
+            te.matmul(T["acc%d" % h][:, 0:HW], T["lp%d" % r][:], T["lb%d" % r][:, h * HW:(h + 1) * HW], start=(i == 0),
                       stop=(i == d - 1)).then_inc(sem["am%d" % h], 1)
 
     ve.wait_ge(sem.ldB, 16)

@@ -3,21 +3,26 @@ from concourse.mybir import AluOpType
 N = 5
 W = 512
 TW = 128
-HW = 256
+NQ = 4
+QW = W // NQ
+HW = W // 2
 WORLD = 256
+LAST = N - 2
 
-BD = {0: [4, 3], 1: [3, 2], 2: [4], 3: []}
-BR = {0: [2, 1], 1: [4], 2: [3], 3: [4]}
+BD = {0: [3, 2], 1: [3, 2], 2: [4], 3: [4]}
+BR = {0: [4, 1], 1: [4], 2: [3]}
+TURN = [(2, 0)]
 
 SCRATCH = {"own": ("sbuf", [128, W + TW * (N - 1)], "bfloat16"),
            "ones": ("sbuf", [128, TW], "bfloat16"),
            "zero": ("sbuf", [128, TW], "bfloat16"),
            "ident": ("sbuf", [128, TW], "bfloat16"),
            "yo": ("sbuf", [128, W], "bfloat16"),
+           "lq": ("sbuf", [128, TW], "bfloat16"),
            "acc0": ("psum", [128, W], "float32"),
            "acc1": ("psum", [128, W], "float32")}
 for _s in range(N - 1):
-    SCRATCH["lb%d" % _s] = ("sbuf", [128, W], "bfloat16")
+    SCRATCH["lb%d" % _s] = ("sbuf", [128, W + (TW if _s == LAST else 0)], "bfloat16")
     SCRATCH["lp%d" % _s] = ("sbuf", [128, TW], "bfloat16")
 for _q in range(1, N - 1):
     SCRATCH["rt%d" % _q] = ("sbuf", [128, TW * (N - 1 - _q)], "bfloat16")
@@ -27,7 +32,10 @@ for _d in range(2, N):
     SCRATCH["Pp%d" % _d] = ("sbuf", [128, TW], "bfloat16")
     SCRATCH["pp%d" % _d] = ("psum", [128, W], "float32")
 
-SEMAPHORES = (["ldT", "ldB", "fT", "fB", "sent", "st", "on", "zr", "idn", "am0", "am1", "vs"]
+ACC = ["acc0", "acc1", "pn1", "pp2"]
+
+SEMAPHORES = (["ldT", "ldB", "fT", "fB", "sent", "st", "st1", "on", "zr", "idn", "vs0", "vs1", "tm", "tv"]
+              + ["am%d" % h for h in range(NQ)]
               + [p + "%d" % s for s in range(N - 1) for p in ("arrB", "arrP")]
               + [p + "%d" % q for q in range(1, N - 1) for p in ("arrR", "nm", "nv")]
               + [p + "%d" % d for d in range(2, N) for p in ("pm", "pv")])
@@ -38,6 +46,8 @@ def _count(mask):
 
 
 def _helper(topo, cores, s):
+    if s not in BR:
+        return None
     c = cores[s]
     for x in range(WORLD):
         if (x not in cores and topo.host(x) == topo.host(c) and topo.chip(x) == topo.chip(c)
@@ -58,7 +68,7 @@ def rank_program(g, core, T, topo):
         return _count(mask)
 
     if me is None:
-        for s in range(N - 1):
+        for s in BR:
             if _helper(topo, cores, s) == core:
                 fed = _count(topo.mask(cores[s], core) & ~topo.mask(cores[s], cores[s + 1]))
                 g.wait_ge(sem.fT, fed)
@@ -74,7 +84,7 @@ def rank_program(g, core, T, topo):
     chain = me <= N - 3
 
     if me < N - 1:
-        g.scalar.dma_start(T.own[:, W:W + TW * (N - 1 - me)], T.l[:, TW * (me + 1):TW * N]).then_inc(sem.ldT, 16)
+        g.sync.dma_start(T.own[:, W:W + TW * (N - 1 - me)], T.l[:, TW * (me + 1):TW * N]).then_inc(sem.ldT, 16)
     g.sync.dma_start(T.own[:, 0:W], T.b[:]).then_inc(sem.ldB, 16)
 
     if chain:
@@ -85,22 +95,30 @@ def rank_program(g, core, T, topo):
 
     left = 0
     if me < N - 1:
-        hc = _helper(topo, cores, me)
-        hrid, hpid = topo.addr(hc, core)
-        hmask = topo.mask(core, hc) & ~topo.mask(core, cores[me + 1])
         g.wait_ge(sem.ldT, 16)
-        for lo in range(me):
+        for lo in range(me - 1, -1, -1):
             left += send(lo, T["rt%d" % me][:], T.own[:, W:W + TW * (N - 1 - me)], sem["arrR%d" % me])
-        g.remote_dma(T.own[:, W:W + TW], T.own[:, W:W + TW], sem.fT, sem.sent, hpid, hrid, hmask)
-        left += _count(hmask)
-        g.wait_ge(sem.ldB, 16)
-        g.remote_dma(T.own[:, 0:W], T.own[:, 0:W], sem.fB, sem.sent, hpid, hrid, hmask)
-        left += _count(hmask)
-        for d in BD[me]:
-            left += send(d, T["lb%d" % me][:], T.own[:, 0:W], sem["arrB%d" % me])
+        if me in BR:
+            hc = _helper(topo, cores, me)
+            hrid, hpid = topo.addr(hc, core)
+            hmask = topo.mask(core, hc) & ~topo.mask(core, cores[me + 1])
+            g.remote_dma(T.own[:, W:W + TW], T.own[:, W:W + TW], sem.fT, sem.sent, hpid, hrid, hmask)
+            left += _count(hmask)
+            g.wait_ge(sem.ldB, 16)
+            g.remote_dma(T.own[:, 0:W], T.own[:, 0:W], sem.fB, sem.sent, hpid, hrid, hmask)
+            left += _count(hmask)
+            for d in BD[me]:
+                left += send(d, T["lb%d" % me][:], T.own[:, 0:W], sem["arrB%d" % me])
+        else:
+            g.wait_ge(sem.ldB, 16)
+            left += send(me + 1, T["lb%d" % me][:], T.own[:, 0:W + TW], sem["arrB%d" % me])
         for d in range(me + 2, N):
-            g.wait_ge(sem["pv%d" % d], 1)
-            left += send(d, T["lp%d" % me][:], T["Pp%d" % d][:], sem["arrP%d" % me])
+            if (d, me) in TURN:
+                g.wait_ge(sem["nv%d" % d], 1)
+                left += send(d, T.lq[:], T["Nn%d" % d][:], sem["arrP%d" % me])
+            else:
+                g.wait_ge(sem["pv%d" % d], 1)
+                left += send(d, T["lp%d" % me][:], T["Pp%d" % d][:], sem["arrP%d" % me])
         g.wait_ge(sem.sent, left)
 
     def tile(d, q):
@@ -119,12 +137,14 @@ def rank_program(g, core, T, topo):
         for p in range(s + 1, N - 1):
             te.wait_ge(sem["nv%d" % p], 1)
             te.wait_ge(sem["arrR%d" % p], _count(topo.mask(cores[p], core)))
-            for k in range(p + 1, N):
-                if k < N - 1:
-                    te.matmul(T["pn%d" % k][:, 0:TW], tile(k, p), T["Nn%d" % p][:], start=False,
-                              stop=(k == p + 1)).then_inc(sem["nm%d" % k], 1)
-                te.matmul(T["pp%d" % k][:, 0:TW], T["Nn%d" % p][:], tile(k, p), start=(p == s + 1),
-                          stop=(k == p + 1)).then_inc(sem["pm%d" % k], 1)
+            for k in range(p + 1, N - 1):
+                te.matmul(T["pn%d" % k][:, 0:TW], tile(k, p), T["Nn%d" % p][:], start=False,
+                          stop=(k == p + 1)).then_inc(sem["nm%d" % k], 1)
+            for k in range(s + 2, N):
+                for q in range(s + 1, k):
+                    if (k, s) not in TURN and max(q, k - 2) == p:
+                        te.matmul(T["pp%d" % k][:, 0:TW], T["Nn%d" % q][:], tile(k, q), start=(q == s + 1),
+                                  stop=(q == k - 1)).then_inc(sem["pm%d" % k], 1)
         ve.wait_ge(sem.zr, 1)
         ve.wait_ge(sem.ldT, 16)
         for k in range(s + 1, N):
@@ -132,7 +152,7 @@ def rank_program(g, core, T, topo):
                 ve.wait_ge(sem["nm%d" % k], k - s)
                 ve.tensor_tensor(T["Nn%d" % k][:], T.zero[:], T["pn%d" % k][:, 0:TW], AluOpType.subtract).then_inc(
                     sem["nv%d" % k], 1)
-            if k > s + 1:
+            if k > s + 1 and (k, s) not in TURN:
                 ve.wait_ge(sem["pm%d" % k], k - 1 - s)
                 ve.tensor_tensor(T["Pp%d" % k][:], tile(k, s), T["pp%d" % k][:, 0:TW], AluOpType.add).then_inc(
                     sem["pv%d" % k], 1)
@@ -144,21 +164,37 @@ def rank_program(g, core, T, topo):
         return
 
     d = me
+    for r in range(d):
+        if (d, r) in TURN:
+            te.wait_ge(sem["arrP%d" % r], _count(topo.mask(cores[r], core)))
+            te.matmul(T.pn2[:, 0:TW], T.lq[:], T.ident[:], start=True, stop=True).then_inc(sem.tm, 1)
+            ve.wait_ge(sem.tm, 1)
+            ve.tensor_tensor(T["lp%d" % r][:], T.zero[:], T.pn2[:, 0:TW], AluOpType.subtract).then_inc(sem.tv, 1)
     for i, r in enumerate(range(d - 1, -1, -1)):
-        psrc = _helper(topo, cores, r) if d == r + 1 else cores[r]
         bsrc = cores[r] if d in BD[r] else _helper(topo, cores, r)
-        te.wait_ge(sem["arrP%d" % r], _count(topo.mask(psrc, core)))
+        if (d, r) in TURN:
+            te.wait_ge(sem.tv, 1)
+            lp = T["lp%d" % r][:]
+        elif r in BR:
+            psrc = _helper(topo, cores, r) if d == r + 1 else cores[r]
+            te.wait_ge(sem["arrP%d" % r], _count(topo.mask(psrc, core)))
+            lp = T["lp%d" % r][:]
+        else:
+            lp = T["lb%d" % r][:, W:W + TW]
         te.wait_ge(sem["arrB%d" % r], _count(topo.mask(bsrc, core)))
-        for h in range(2):
-            te.matmul(T["acc%d" % h][:, 0:HW], T["lp%d" % r][:], T["lb%d" % r][:, h * HW:(h + 1) * HW], start=(i == 0),
+        for h in range(NQ):
+            te.matmul(T[ACC[h]][:, 0:QW], lp, T["lb%d" % r][:, h * QW:(h + 1) * QW], start=(i == 0),
                       stop=(i == d - 1)).then_inc(sem["am%d" % h], 1)
 
     ve.wait_ge(sem.ldB, 16)
-    for h in range(2):
+    for h in range(NQ):
         ve.wait_ge(sem["am%d" % h], d)
-        ve.tensor_tensor(T.yo[:, h * HW:(h + 1) * HW], T.own[:, h * HW:(h + 1) * HW], T["acc%d" % h][:, 0:HW],
-                         AluOpType.subtract).then_inc(sem.vs, 1)
+        ve.tensor_tensor(T.yo[:, h * QW:(h + 1) * QW], T.own[:, h * QW:(h + 1) * QW], T[ACC[h]][:, 0:QW],
+                         AluOpType.subtract).then_inc(sem["vs%d" % (h * QW // HW)], 1)
 
-    g.sync.wait_ge(sem.vs, 2)
-    g.sync.dma_start(T.y[:], T.yo[:]).then_inc(sem.st, 16)
-    g.sync.wait_ge(sem.st, 16)
+    g.scalar.wait_ge(sem.vs0, HW // QW)
+    g.scalar.dma_start(T.y[:, 0:HW], T.yo[:, 0:HW]).then_inc(sem.st, 16)
+    g.sync.wait_ge(sem.vs1, HW // QW)
+    g.sync.dma_start(T.y[:, HW:W], T.yo[:, HW:W]).then_inc(sem.st1, 16)
+    g.scalar.wait_ge(sem.st, 16)
+    g.sync.wait_ge(sem.st1, 16)

from concourse.mybir import AluOpType

N = 5
W = 512
TW = 128
NQ = 4
QW = W // NQ
HW = W // 2
WORLD = 256
LAST = N - 2

BD = {0: [3, 2], 1: [3, 2], 2: [4], 3: [4]}
BR = {0: [4, 1], 1: [4], 2: [3]}
TURN = [(2, 0)]

SCRATCH = {"own": ("sbuf", [128, W + TW * (N - 1)], "bfloat16"),
           "ones": ("sbuf", [128, TW], "bfloat16"),
           "zero": ("sbuf", [128, TW], "bfloat16"),
           "ident": ("sbuf", [128, TW], "bfloat16"),
           "yo": ("sbuf", [128, W], "bfloat16"),
           "lq": ("sbuf", [128, TW], "bfloat16"),
           "acc0": ("psum", [128, W], "float32"),
           "acc1": ("psum", [128, W], "float32")}
for _s in range(N - 1):
    SCRATCH["lb%d" % _s] = ("sbuf", [128, W + (TW if _s == LAST else 0)], "bfloat16")
    SCRATCH["lp%d" % _s] = ("sbuf", [128, TW], "bfloat16")
for _q in range(1, N - 1):
    SCRATCH["rt%d" % _q] = ("sbuf", [128, TW * (N - 1 - _q)], "bfloat16")
    SCRATCH["Nn%d" % _q] = ("sbuf", [128, TW], "bfloat16")
    SCRATCH["pn%d" % _q] = ("psum", [128, W], "float32")
for _d in range(2, N):
    SCRATCH["Pp%d" % _d] = ("sbuf", [128, TW], "bfloat16")
    SCRATCH["pp%d" % _d] = ("psum", [128, W], "float32")

ACC = ["acc0", "acc1", "pn1", "pp2"]

SEMAPHORES = (["ldT", "ldB", "fT", "fB", "sent", "st", "st1", "on", "zr", "idn", "vs0", "vs1", "tm", "tv"]
              + ["am%d" % h for h in range(NQ)]
              + [p + "%d" % s for s in range(N - 1) for p in ("arrB", "arrP")]
              + [p + "%d" % q for q in range(1, N - 1) for p in ("arrR", "nm", "nv")]
              + [p + "%d" % d for d in range(2, N) for p in ("pm", "pv")])


def _count(mask):
    return bin(mask).count("1")


def _helper(topo, cores, s):
    if s not in BR:
        return None
    c = cores[s]
    for x in range(WORLD):
        if (x not in cores and topo.host(x) == topo.host(c) and topo.chip(x) == topo.chip(c)
                and topo.die(x) != topo.die(c) and all(topo.may_write(x, cores[d]) for d in BR[s] + [s + 1])):
            return x
    return None


def rank_program(g, core, T, topo):
    sem = T.sem
    cores = list(T.cores)
    me = T.rank_of(core)

    def send(d, out_ap, in_ap, rsem):
        rid, pid = topo.addr(cores[d], core)
        mask = topo.mask(core, cores[d])
        g.remote_dma(out_ap, in_ap, rsem, sem.sent, pid, rid, mask)
        return _count(mask)

    if me is None:
        for s in BR:
            if _helper(topo, cores, s) == core:
                fed = _count(topo.mask(cores[s], core) & ~topo.mask(cores[s], cores[s + 1]))
                g.wait_ge(sem.fT, fed)
                left = send(s + 1, T["lp%d" % s][:], T.own[:, W:W + TW], sem["arrP%d" % s])
                g.wait_ge(sem.fB, fed)
                for d in BR[s]:
                    left += send(d, T["lb%d" % s][:], T.own[:, 0:W], sem["arrB%d" % s])
                g.wait_ge(sem.sent, left)
        return

    s = me
    te, ve = g.tensor, g.vector
    chain = me <= N - 3

    if me < N - 1:
        g.sync.dma_start(T.own[:, W:W + TW * (N - 1 - me)], T.l[:, TW * (me + 1):TW * N]).then_inc(sem.ldT, 16)
    g.sync.dma_start(T.own[:, 0:W], T.b[:]).then_inc(sem.ldB, 16)

    if chain:
        ve.memset(T.ones[:], 1.0).then_inc(sem.on, 1)
        ve.memset(T.zero[:], 0.0).then_inc(sem.zr, 1)
        g.wait_ge(sem.on, 1)
        g.affine_select(T.ident[:], T.ones[:], [[-1, TW]], AluOpType.is_equal, 0.0, 0, 1).then_inc(sem.idn, 1)

    left = 0
    if me < N - 1:
        g.wait_ge(sem.ldT, 16)
        for lo in range(me - 1, -1, -1):
            left += send(lo, T["rt%d" % me][:], T.own[:, W:W + TW * (N - 1 - me)], sem["arrR%d" % me])
        if me in BR:
            hc = _helper(topo, cores, me)
            hrid, hpid = topo.addr(hc, core)
            hmask = topo.mask(core, hc) & ~topo.mask(core, cores[me + 1])
            g.remote_dma(T.own[:, W:W + TW], T.own[:, W:W + TW], sem.fT, sem.sent, hpid, hrid, hmask)
            left += _count(hmask)
            g.wait_ge(sem.ldB, 16)
            g.remote_dma(T.own[:, 0:W], T.own[:, 0:W], sem.fB, sem.sent, hpid, hrid, hmask)
            left += _count(hmask)
            for d in BD[me]:
                left += send(d, T["lb%d" % me][:], T.own[:, 0:W], sem["arrB%d" % me])
        else:
            g.wait_ge(sem.ldB, 16)
            left += send(me + 1, T["lb%d" % me][:], T.own[:, 0:W + TW], sem["arrB%d" % me])
        for d in range(me + 2, N):
            if (d, me) in TURN:
                g.wait_ge(sem["nv%d" % d], 1)
                left += send(d, T.lq[:], T["Nn%d" % d][:], sem["arrP%d" % me])
            else:
                g.wait_ge(sem["pv%d" % d], 1)
                left += send(d, T["lp%d" % me][:], T["Pp%d" % d][:], sem["arrP%d" % me])
        g.wait_ge(sem.sent, left)

    def tile(d, q):
        if q == me:
            c = W + TW * (d - me - 1)
            return T.own[:, c:c + TW]
        c = TW * (d - q - 1)
        return T["rt%d" % q][:, c:c + TW]

    if chain:
        te.wait_ge(sem.idn, 1)
        te.wait_ge(sem.ldT, 16)
        for q in range(s + 1, N - 1):
            te.matmul(T["pn%d" % q][:, 0:TW], tile(q, s), T.ident[:], start=True, stop=(q == s + 1)).then_inc(
                sem["nm%d" % q], 1)
        for p in range(s + 1, N - 1):
            te.wait_ge(sem["nv%d" % p], 1)
            te.wait_ge(sem["arrR%d" % p], _count(topo.mask(cores[p], core)))
            for k in range(p + 1, N - 1):
                te.matmul(T["pn%d" % k][:, 0:TW], tile(k, p), T["Nn%d" % p][:], start=False,
                          stop=(k == p + 1)).then_inc(sem["nm%d" % k], 1)
            for k in range(s + 2, N):
                for q in range(s + 1, k):
                    if (k, s) not in TURN and max(q, k - 2) == p:
                        te.matmul(T["pp%d" % k][:, 0:TW], T["Nn%d" % q][:], tile(k, q), start=(q == s + 1),
                                  stop=(q == k - 1)).then_inc(sem["pm%d" % k], 1)
        ve.wait_ge(sem.zr, 1)
        ve.wait_ge(sem.ldT, 16)
        for k in range(s + 1, N):
            if k < N - 1:
                ve.wait_ge(sem["nm%d" % k], k - s)
                ve.tensor_tensor(T["Nn%d" % k][:], T.zero[:], T["pn%d" % k][:, 0:TW], AluOpType.subtract).then_inc(
                    sem["nv%d" % k], 1)
            if k > s + 1 and (k, s) not in TURN:
                ve.wait_ge(sem["pm%d" % k], k - 1 - s)
                ve.tensor_tensor(T["Pp%d" % k][:], tile(k, s), T["pp%d" % k][:, 0:TW], AluOpType.add).then_inc(
                    sem["pv%d" % k], 1)

    if me == 0:
        g.scalar.wait_ge(sem.sent, left)
        g.scalar.dma_start(T.y[:], T.own[:, 0:W]).then_inc(sem.st, 16)
        g.scalar.wait_ge(sem.st, 16)
        return

    d = me
    for r in range(d):
        if (d, r) in TURN:
            te.wait_ge(sem["arrP%d" % r], _count(topo.mask(cores[r], core)))
            te.matmul(T.pn2[:, 0:TW], T.lq[:], T.ident[:], start=True, stop=True).then_inc(sem.tm, 1)
            ve.wait_ge(sem.tm, 1)
            ve.tensor_tensor(T["lp%d" % r][:], T.zero[:], T.pn2[:, 0:TW], AluOpType.subtract).then_inc(sem.tv, 1)
    for i, r in enumerate(range(d - 1, -1, -1)):
        bsrc = cores[r] if d in BD[r] else _helper(topo, cores, r)
        if (d, r) in TURN:
            te.wait_ge(sem.tv, 1)
            lp = T["lp%d" % r][:]
        elif r in BR:
            psrc = _helper(topo, cores, r) if d == r + 1 else cores[r]
            te.wait_ge(sem["arrP%d" % r], _count(topo.mask(psrc, core)))
            lp = T["lp%d" % r][:]
        else:
            lp = T["lb%d" % r][:, W:W + TW]
        te.wait_ge(sem["arrB%d" % r], _count(topo.mask(bsrc, core)))
        for h in range(NQ):
            te.matmul(T[ACC[h]][:, 0:QW], lp, T["lb%d" % r][:, h * QW:(h + 1) * QW], start=(i == 0),
                      stop=(i == d - 1)).then_inc(sem["am%d" % h], 1)

    ve.wait_ge(sem.ldB, 16)
    for h in range(NQ):
        ve.wait_ge(sem["am%d" % h], d)
        ve.tensor_tensor(T.yo[:, h * QW:(h + 1) * QW], T.own[:, h * QW:(h + 1) * QW], T[ACC[h]][:, 0:QW],
                         AluOpType.subtract).then_inc(sem["vs%d" % (h * QW // HW)], 1)

    g.scalar.wait_ge(sem.vs0, HW // QW)
    g.scalar.dma_start(T.y[:, 0:HW], T.yo[:, 0:HW]).then_inc(sem.st, 16)
    g.sync.wait_ge(sem.vs1, HW // QW)
    g.sync.dma_start(T.y[:, HW:W], T.yo[:, HW:W]).then_inc(sem.st1, 16)
    g.scalar.wait_ge(sem.st, 16)
    g.sync.wait_ge(sem.st1, 16)
